import numpy as np
import ml_dtypes


def mxq(x, axis, fmt="e4m3"):
    dtype, down = {"e4m3": (ml_dtypes.float8_e4m3fn, 7), "e5m2": (ml_dtypes.float8_e5m2, 14)}[fmt]
    v = np.moveaxis(np.asarray(x, np.float32).astype(ml_dtypes.bfloat16).astype(np.float64), axis, -1)
    blocks = v.reshape(v.shape[:-1] + (-1, 32))
    amax = np.abs(blocks).max(-1, keepdims=True)
    byte = np.maximum(np.where(amax > 0, np.frexp(amax)[1] - 1 + 127, 0) - down, 1)
    scale = np.exp2(byte - 127.0)
    codes = (blocks / scale).astype(np.float32).astype(dtype).astype(np.float64)
    return np.moveaxis((codes * scale).reshape(v.shape), -1, axis)


WIDE = False


def mx_kscale(k):
    if not WIDE:
        return np.ones(k)
    levels = np.array([30, -30])
    if k % 512:
        return np.exp2(np.random.permutation(np.resize(levels, k // 32))).repeat(32)
    a = np.empty((k // 512, 16))
    for p in range(k // 512):
        a[p, :8] = np.random.permutation(np.resize(levels, 8))
        for g in range(8):
            far = levels[np.abs(levels - a[p, g]) >= 10]
            a[p, g + 8] = far[np.random.randint(len(far))]
    return np.exp2(a.ravel()).repeat(32)


def f64(x):
    return np.asarray(x).astype(np.float64)


def striped(idx):
    return np.tile(np.asarray(idx).reshape(-1, 16).T, (8, 1)).astype(np.uint16)


def unstriped(offs):
    return offs[:16].T.reshape(-1).astype(np.int64)


E2M1 = np.array([0.0, 0.5, 1.0, 1.5, 2.0, 3.0, 4.0, 6.0, -0.0, -0.5, -1.0, -1.5, -2.0, -3.0, -4.0, -6.0])


def pack_weight(w, fmt):
    k, n = w.shape
    w = f64(np.asarray(w, np.float32).astype(ml_dtypes.bfloat16)).reshape(k // 32, 32, n)
    amax = np.abs(w).max(1)
    if fmt in ("e4m3", "e5m2"):
        byte = np.frexp(amax)[1] - 1 + 127 - (7 if fmt == "e4m3" else 14)
    else:
        mant, ex = np.frexp(amax / 6.0)
        byte = np.where(mant > 0.5, ex, ex - 1) + 127
    byte = np.clip(np.where(amax > 0, byte, 1), 1, 254)
    scaled = (w * np.exp2(127.0 - byte)[:, None, :]).reshape(k, n).astype(np.float32)
    by_word = np.ascontiguousarray(scaled.reshape(k // 512, 128, 4, n).transpose(0, 1, 3, 2))
    if fmt in ("e4m3", "e5m2"):
        words = by_word.astype(ml_dtypes.float8_e4m3fn if fmt == "e4m3" else ml_dtypes.float8_e5m2).view(np.uint8)
    else:
        c = by_word.astype(ml_dtypes.float4_e2m1fn).view(np.uint8) & 0xF
        words = (c[..., 0::2] | (c[..., 1::2] << 4)).reshape(k // 512, 128, 2 * n)
    return np.ascontiguousarray(words), np.ascontiguousarray(byte.astype(np.uint8).reshape(k // 512, 16, n))


def unpack_weight(words, scales, fmt):
    g, _, n = scales.shape
    words = np.ascontiguousarray(words).reshape(g, 128, n, -1)
    if fmt in ("e4m3", "e5m2"):
        vals = words.view(ml_dtypes.float8_e4m3fn if fmt == "e4m3" else ml_dtypes.float8_e5m2).astype(np.float64)
    else:
        nib = np.empty((g, 128, n, 4), np.uint8)
        nib[..., 0::2] = words & 0xF
        nib[..., 1::2] = words >> 4
        vals = E2M1[nib]
    vals = vals * np.repeat(np.exp2(scales.astype(np.float64) - 127.0), 8, axis=1)[..., None]
    return vals.transpose(0, 1, 3, 2).reshape(g * 512, n)


def sgn(shape):
    return np.random.uniform(0.5, 2.0, shape) * np.where(np.random.standard_normal(shape) < 0, -1.0, 1.0)


K, T, J, R, C, D, O, N = 512, 2048, 256, 512, 512, 512, 256, 256


def setup_inputs():
    n = np.random.standard_normal
    idx = np.random.permutation(T)[:J]
    idx2 = np.random.permutation(T)[:J]
    idx3 = np.random.permutation(C)[:J]
    idx4 = np.random.permutation(C)[:J]
    idx5 = np.random.permutation(D)[:J]
    idx6 = np.random.permutation(D)[:O]
    fk = mx_kscale(K)
    fr = mx_kscale(R)
    xtp = pack_weight(n((K, T)) / fk[:, None], "e5m2")
    wp = pack_weight(n((K, R)) * 1 / np.sqrt(K) * fk[:, None], "e2m1")
    w2p = pack_weight(n((K, R)) * 1 / np.sqrt(K) * fk[:, None], "e4m3")
    wbp = pack_weight(n((R, N)) * 1 / np.sqrt(R) / fr[:, None], "e2m1")
    return {
        "xt_words": xtp[0],
        "xt_scales": xtp[1],
        "w_words": wp[0],
        "w_scales": wp[1],
        "w2_words": w2p[0],
        "w2_scales": w2p[1],
        "sa": (sgn((R, 1))).astype(np.float32),
        "sb": (np.random.uniform(0.5, 1.6, (R, 1)) * fr[:, None]).astype(np.float32),
        "wb_words": wbp[0],
        "wb_scales": wbp[1],
        "offs": striped(idx),
        "offs2": striped(idx2),
        "offs3": striped(idx3),
        "offs4": striped(idx4),
        "offs5": striped(idx5),
        "offs6": striped(idx6),
    }


def reference(xt_words, xt_scales, w_words, w_scales, w2_words, w2_scales, sa, sb, wb_words, wb_scales, offs, offs2, offs3, offs4, offs5, offs6):
    idx = unstriped(offs)
    idx2 = unstriped(offs2)
    idx3 = unstriped(offs3)
    idx4 = unstriped(offs4)
    idx5 = unstriped(offs5)
    idx6 = unstriped(offs6)
    xtu = unpack_weight(xt_words, xt_scales, "e5m2")
    wu = unpack_weight(w_words, w_scales, "e2m1")
    w2u = unpack_weight(w2_words, w2_scales, "e4m3")
    wbu = unpack_weight(wb_words, wb_scales, "e2m1")
    xtidxg = xtu[:, idx]
    a = wu.T @ xtidxg
    xtidx2g = xtu[:, idx2]
    b = w2u.T @ xtidx2g
    pa = np.zeros((R, C))
    pa[:, idx3] = a * f64(sa)
    h1 = np.abs(pa[:, idx4] - b)
    pb = np.zeros((R, D))
    pb[:, idx5] = h1 * f64(sb)
    hid = pb[:, idx6]
    hidq = mxq(hid, 0, "e4m3")
    p = wbu.T @ hidq
    return p

@@ -1,0 +1,192 @@
+from contextlib import ExitStack
+
+import concourse.mybir as mybir
+
+K, T, J, R, C, D, O, N = 512, 2048, 256, 512, 512, 512, 256, 256
+FLOPS = 2 * (2 * K * R * J + R * N * O)
+
+F32 = mybir.dt.float32
+BF16 = mybir.dt.bfloat16
+I32 = mybir.dt.int32
+U32 = mybir.dt.uint32
+U16 = mybir.dt.uint16
+U8 = mybir.dt.uint8
+E4M3 = mybir.dt.float8_e4m3fn_x4
+E5M2 = mybir.dt.float8_e5m2_x4
+E2M1 = mybir.dt.float4_e2m1fn_x4
+COPY = mybir.ActivationFunctionType.Copy
+ALU = mybir.AluOpType
+
+P = 128
+PACK = 4
+HALF = 128
+LIST_HALF = HALF // 16
+
+
+def tile_list_relayed_kernel(tc, xt_words, xt_scales, w_words, w_scales, w2_words, w2_scales, sa, sb,
+                                 wb_words, wb_scales, offs, offs2, offs3, offs4, offs5, offs6, out):
+    nc = tc.nc
+    with ExitStack() as ctx:
+        lists = ctx.enter_context(tc.tile_pool(name="lists", bufs=1))
+        sbuf = ctx.enter_context(tc.tile_pool(name="sbuf", bufs=1))
+        psum = ctx.enter_context(tc.psum_pool(name="psum", bufs=1))
+
+        def load_list(src, name):
+            t = lists.tile([P, J // 16], U16, name=name)
+            nc.sync.dma_start(t[:], src)
+            return t
+
+        def half(lst, h):
+            return lst[:, h * LIST_HALF:(h + 1) * LIST_HALF]
+
+        def zero_plane(width, name):
+            t = sbuf.tile([P, 2 * width], U8, name=name, align_bytes=64)
+            nc.vector.memset(t[0:64, :].bitcast(I32), 0)
+            return t
+
+        def load_plane(plane, scales, width):
+            rows = scales[0].rearrange("(u q r) n -> q r u n", u=2, q=2)
+            for q in range(2):
+                nc.sync.dma_start(plane[32 * q:32 * q + 4, :].bitcast(I32).rearrange("r (u n) -> r u n", u=2),
+                                  rows[q].bitcast(I32))
+
+        def spread_plane(plane, width):
+            nc.vector.tensor_copy(plane[64:128, 0:width].bitcast(I32), plane[0:64, width:2 * width].bitcast(I32))
+
+        xs = sbuf.tile([P, T], U8, name="xs")
+        nc.vector.memset(xs[:].bitcast(I32), 0)
+        ws_raw = zero_plane(R, "ws_raw")
+
+        l1 = load_list(offs, "l1")
+        l3 = load_list(offs3, "l3")
+        l4 = load_list(offs4, "l4")
+        l5 = load_list(offs5, "l5")
+        w_raw = sbuf.tile([P, 2 * R], U8, name="w_raw")
+        nc.scalar.dma_start(w_raw[:].bitcast(I32), w_words[0].bitcast(I32))
+        sa_t = sbuf.tile([P, PACK], F32, name="sa_t")
+        nc.scalar.dma_start(sa_t[:], sa.rearrange("(p t) o -> p (t o)", t=PACK))
+        sb_t = sbuf.tile([P, PACK], F32, name="sb_t")
+        nc.scalar.dma_start(sb_t[:], sb.rearrange("(p t) o -> p (t o)", t=PACK))
+        xw = sbuf.tile([P, T], U32, name="xw")
+        nc.scalar.dma_start(xw[:].bitcast(I32), xt_words[0].rearrange("p c b -> p (c b)").bitcast(I32))
+        for q in range(4):
+            nc.sync.dma_start(xs[32 * q:32 * q + 4, :].bitcast(I32), xt_scales[0, 4 * q:4 * q + 4, :].bitcast(I32))
+        load_plane(ws_raw, w_scales, R)
+
+        pa = [sbuf.tile([P, C], F32, name="pa%d" % t) for t in range(PACK)]
+        for t in range(PACK):
+            nc.vector.memset(pa[t][:], 0.0)
+
+        w2s_raw = zero_plane(R, "w2s_raw")
+        wbs = zero_plane(N, "wbs")
+        l2 = load_list(offs2, "l2")
+        w2_raw = sbuf.tile([P, R], U32, name="w2_raw")
+        nc.sync.dma_start(w2_raw[:].bitcast(I32), w2_words[0].rearrange("p c b -> p (c b)").bitcast(I32))
+        load_plane(w2s_raw, w2_scales, R)
+        wb = sbuf.tile([P, 2 * N], U8, name="wb", align_bytes=64)
+        nc.sync.dma_start(wb[:].bitcast(I32), wb_words[0].bitcast(I32))
+        load_plane(wbs, wb_scales, N)
+        l6 = load_list(offs6, "l6")
+
+        w_dealt = sbuf.tile([P, 2 * R], U8, name="w_dealt", align_bytes=64)
+        nc.scalar.copy(w_dealt[:].bitcast(U16).rearrange("p (t m) -> p t m", t=PACK),
+                       w_raw[:].bitcast(U16).rearrange("p (m t) -> p t m", t=PACK))
+        spread_plane(ws_raw, R)
+        ws_dealt = sbuf.tile([P, R], U8, name="ws_dealt", align_bytes=64)
+        nc.vector.tensor_copy(ws_dealt[:].rearrange("p (t m) -> p t m", t=PACK),
+                              ws_raw[:, 0:R].rearrange("p (m t) -> p t m", t=PACK))
+        x1s = sbuf.tile([P, J], U8, name="x1s", align_bytes=64)
+        nc.vector.tensor_copy(x1s[:], xs[:].indirect(l1[:]))
+        x1w = sbuf.tile([P, J], U32, name="x1w", align_bytes=64)
+        for h in range(2):
+            nc.vector.tensor_copy(x1w[:, h * HALF:(h + 1) * HALF], xw[:].indirect(half(l1, h)))
+
+        def product_a(dst, t, j0, j1):
+            nc.tensor.matmul_mx(out=dst, lhsT=w_dealt[:, 2 * P * t:2 * P * (t + 1)].bitcast(E2M1),
+                                lhsT_scale=ws_dealt[:, P * t:P * (t + 1)],
+                                rhs=x1w[:, j0:j1].bitcast(E5M2), rhs_scale=x1s[:, j0:j1], start=True, stop=True)
+
+        a_first = []
+        for t in range(2):
+            bank = psum.tile([P, HALF], F32, name="bank%d" % t)
+            product_a(bank[:], t, 0, HALF)
+            s = sbuf.tile([P, HALF], F32, name="a_first%d" % t, align_bytes=64)
+            nc.scalar.activation(out=s[:], in_=bank[:], func=COPY)
+            a_first.append(s)
+        bank2 = psum.tile([P, 2, HALF], F32, name="bank2")
+        for t in range(2):
+            product_a(bank2[:, t, :], t, HALF, J)
+        a_second = sbuf.tile([P, 2, HALF], F32, name="a_second")
+        nc.vector.tensor_copy(a_second[:], bank2[:])
+        bank3 = psum.tile([P, 2, J], F32, name="bank3")
+        for t in range(2):
+            product_a(bank3[:, t, :], 2 + t, 0, J)
+        a_rest = sbuf.tile([P, 2, J], F32, name="a_rest")
+        nc.vector.tensor_copy(a_rest[:], bank3[:])
+
+        def put(board, offsets, src, scale):
+            nc.scalar.activation(out=board[:].indirect(offsets), in_=src, func=COPY, scale=scale)
+
+        for t in range(2):
+            put(pa[t], half(l3, 0), a_first[t][:], sa_t[:, t:t + 1])
+        for t in range(2):
+            put(pa[t], half(l3, 1), a_second[:, t, :], sa_t[:, t:t + 1])
+        for t in range(2):
+            put(pa[2 + t], l3[:], a_rest[:, t, :], sa_t[:, 2 + t:3 + t])
+
+        x2s = sbuf.tile([P, J], U8, name="x2s", tag="a_first0", align_bytes=64)
+        nc.vector.tensor_copy(x2s[:], xs[:].indirect(l2[:]))
+        x2w = sbuf.tile([P, J], U32, name="x2w", align_bytes=64)
+        nc.vector.tensor_copy(x2w[:], xw[:].indirect(l2[:]))
+        w2_dealt = sbuf.tile([P, R], U32, name="w2_dealt", align_bytes=64)
+        nc.vector.tensor_copy(w2_dealt[:].bitcast(I32).rearrange("p (t m) -> p t m", t=PACK),
+                              w2_raw[:].bitcast(I32).rearrange("p (m t) -> p t m", t=PACK))
+        spread_plane(w2s_raw, R)
+        w2s_dealt = sbuf.tile([P, R], U8, name="w2s_dealt", align_bytes=64)
+        nc.vector.tensor_copy(w2s_dealt[:].rearrange("p (t m) -> p t m", t=PACK),
+                              w2s_raw[:, 0:R].rearrange("p (m t) -> p t m", t=PACK))
+        spread_plane(wbs, N)
+        b_banks = []
+        for u in range(2):
+            bank = psum.tile([P, 2, J], F32, name="b_bank%d" % u)
+            for i in range(2):
+                t = 2 * u + i
+                nc.tensor.matmul_mx(out=bank[:, i, :], lhsT=w2_dealt[:, P * t:P * (t + 1)].bitcast(E4M3),
+                                    lhsT_scale=w2s_dealt[:, P * t:P * (t + 1)],
+                                    rhs=x2w[:].bitcast(E5M2), rhs_scale=x2s[:], start=True, stop=True)
+            b_banks.append(bank)
+
+        pb = [sbuf.tile([P, D], F32, name="pb%d" % t, tag=spent, align_bytes=64)
+              for t, spent in enumerate(("w_dealt", "ws_dealt", "w2_dealt", "w2s_dealt"))]
+        for t in range(PACK):
+            picked = sbuf.tile([P, J], F32, name="picked%d" % t, tag="picked", bufs=2)
+            nc.vector.tensor_copy(picked[:], pa[t][:].indirect(l4[:]))
+            nc.vector.memset(pb[t][:], 0.0)
+            diff = sbuf.tile([P, J], F32, name="diff%d" % t, tag="diff")
+            nc.vector.tensor_tensor(diff[:], picked[:], b_banks[t // 2][:, t % 2, :], ALU.subtract)
+            h1 = sbuf.tile([P, J], F32, name="h1_%d" % t)
+            nc.vector.scalar_tensor_tensor(h1[:], diff[:], -1.0, diff[:], ALU.mult, ALU.max)
+            put(pb[t], l5[:], h1[:], sb_t[:, t:t + 1])
+
+        hid = [sbuf.tile([P, HALF * PACK], BF16, name="hid%d" % h, align_bytes=64) for h in range(2)]
+        for t in range(PACK):
+            for h in range(2):
+                nc.scalar.activation(out=hid[h][:, t:HALF * PACK:PACK], in_=pb[t][:].indirect(half(l6, h)), func=COPY)
+
+        out_rows = out.rearrange("(g p) o -> p g o", p=P)
+        for h in range(2):
+            codes = sbuf.tile([P, HALF], U32, name="codes%d" % h, align_bytes=64)
+            plane = sbuf.tile([P, HALF], U8, name="plane%d" % h, align_bytes=64)
+            nc.vector.quantize_mx(out=codes[:].bitcast(E4M3), scales=plane[:], in_=hid[h][:])
+            for g in range(2):
+                bank = psum.tile([P, HALF], F32, name="o_bank%d" % g) if h == 0 else psum.tile([P, HALF], F32, name="o_last%d" % g, tag="bank%d" % g)
+                nc.tensor.matmul_mx(out=bank[:], lhsT=wb[:, 2 * P * g:2 * P * (g + 1)].bitcast(E2M1),
+                                    lhsT_scale=wbs[:, P * g:P * (g + 1)],
+                                    rhs=codes[:].bitcast(E4M3), rhs_scale=plane[:], start=True, stop=True)
+                res = sbuf.tile([P, HALF], F32, name="res%d%d" % (h, g))
+                if g == 1:
+                    nc.scalar.copy(res[:], bank[:])
+                    nc.scalar.dma_start(out_rows[:, g, h * HALF:(h + 1) * HALF], res[:])
+                else:
+                    nc.vector.tensor_copy(res[:], bank[:])
+                    nc.sync.dma_start(out_rows[:, g, h * HALF:(h + 1) * HALF], res[:])

@@ -39,8 +39,8 @@ def tile_list_relayed_kernel(tc, xt_words, xt_scales, w_words, w_scales, w2_word
         def half(lst, h):
             return lst[:, h * LIST_HALF:(h + 1) * LIST_HALF]
 
-        def zero_plane(width, name):
-            t = sbuf.tile([P, 2 * width], U8, name=name, align_bytes=64)
+        def zero_plane(width, name, tag, bufs):
+            t = sbuf.tile([P, 2 * width], U8, name=name, tag=tag, bufs=bufs, align_bytes=64)
             nc.vector.memset(t[0:64, :].bitcast(I32), 0)
             return t
 
@@ -55,7 +55,8 @@ def tile_list_relayed_kernel(tc, xt_words, xt_scales, w_words, w_scales, w2_word
 
         xs = sbuf.tile([P, T], U8, name="xs")
         nc.vector.memset(xs[:].bitcast(I32), 0)
-        ws_raw = zero_plane(R, "ws_raw")
+        ws_raw = sbuf.tile([P, R], U8, name="ws_raw")
+        nc.vector.memset(ws_raw[:].bitcast(I32), 0)
 
         l1 = load_list(offs, "l1")
         l3 = load_list(offs3, "l3")
@@ -63,26 +64,27 @@ def tile_list_relayed_kernel(tc, xt_words, xt_scales, w_words, w_scales, w2_word
         l5 = load_list(offs5, "l5")
         w_raw = sbuf.tile([P, 2 * R], U8, name="w_raw")
         nc.scalar.dma_start(w_raw[:].bitcast(I32), w_words[0].bitcast(I32))
-        sa_t = sbuf.tile([P, PACK], F32, name="sa_t")
-        nc.scalar.dma_start(sa_t[:], sa.rearrange("(p t) o -> p (t o)", t=PACK))
-        sb_t = sbuf.tile([P, PACK], F32, name="sb_t")
-        nc.scalar.dma_start(sb_t[:], sb.rearrange("(p t) o -> p (t o)", t=PACK))
+        ws_rows = sbuf.tile([4, 4, R // 4], I32, name="ws_rows")
+        nc.scalar.dma_start(ws_rows[:], w_scales[0].rearrange("(q r) n -> r q n", q=4).bitcast(I32))
         xw = sbuf.tile([P, T], U32, name="xw")
         nc.scalar.dma_start(xw[:].bitcast(I32), xt_words[0].rearrange("p c b -> p (c b)").bitcast(I32))
         for q in range(4):
             nc.sync.dma_start(xs[32 * q:32 * q + 4, :].bitcast(I32), xt_scales[0, 4 * q:4 * q + 4, :].bitcast(I32))
-        load_plane(ws_raw, w_scales, R)
+        l2 = load_list(offs2, "l2")
+        sa_t = sbuf.tile([P, PACK], F32, name="sa_t")
+        nc.sync.dma_start(sa_t[:], sa.rearrange("(p t) o -> p (t o)", t=PACK))
 
         pa = [sbuf.tile([P, C], F32, name="pa%d" % t) for t in range(PACK)]
         for t in range(PACK):
             nc.vector.memset(pa[t][:], 0.0)
 
-        w2s_raw = zero_plane(R, "w2s_raw")
-        wbs = zero_plane(N, "wbs")
-        l2 = load_list(offs2, "l2")
-        w2_raw = sbuf.tile([P, R], U32, name="w2_raw")
+        w2s_raw = zero_plane(R, "w2s_raw", "picked", 2)
+        wbs = zero_plane(N, "wbs", "wbs", 1)
+        w2_raw = sbuf.tile([P, R], U32, name="w2_raw", tag="picked", bufs=2, align_bytes=64)
         nc.sync.dma_start(w2_raw[:].bitcast(I32), w2_words[0].rearrange("p c b -> p (c b)").bitcast(I32))
         load_plane(w2s_raw, w2_scales, R)
+        sb_t = sbuf.tile([P, PACK], F32, name="sb_t")
+        nc.sync.dma_start(sb_t[:], sb.rearrange("(p t) o -> p (t o)", t=PACK))
         wb = sbuf.tile([P, 2 * N], U8, name="wb", align_bytes=64)
         nc.sync.dma_start(wb[:].bitcast(I32), wb_words[0].bitcast(I32))
         load_plane(wbs, wb_scales, N)
@@ -91,10 +93,11 @@ def tile_list_relayed_kernel(tc, xt_words, xt_scales, w_words, w_scales, w2_word
         w_dealt = sbuf.tile([P, 2 * R], U8, name="w_dealt", align_bytes=64)
         nc.scalar.copy(w_dealt[:].bitcast(U16).rearrange("p (t m) -> p t m", t=PACK),
                        w_raw[:].bitcast(U16).rearrange("p (m t) -> p t m", t=PACK))
-        spread_plane(ws_raw, R)
+        for q in range(4):
+            nc.vector.tensor_copy(ws_raw[32 * q:32 * q + 4, :].bitcast(I32), ws_rows[:, q, :])
         ws_dealt = sbuf.tile([P, R], U8, name="ws_dealt", align_bytes=64)
         nc.vector.tensor_copy(ws_dealt[:].rearrange("p (t m) -> p t m", t=PACK),
-                              ws_raw[:, 0:R].rearrange("p (m t) -> p t m", t=PACK))
+                              ws_raw[:].rearrange("p (m t) -> p t m", t=PACK))
         x1s = sbuf.tile([P, J], U8, name="x1s", align_bytes=64)
         nc.vector.tensor_copy(x1s[:], xs[:].indirect(l1[:]))
         x1w = sbuf.tile([P, J], U32, name="x1w", align_bytes=64)
@@ -157,18 +160,19 @@ def tile_list_relayed_kernel(tc, xt_words, xt_scales, w_words, w_scales, w2_word
             b_banks.append(bank)
 
         pb = [sbuf.tile([P, D], F32, name="pb%d" % t, tag=spent, align_bytes=64)
-              for t, spent in enumerate(("w_dealt", "ws_dealt", "w2_dealt", "w2s_dealt"))]
+              for t, spent in enumerate(("ws_dealt", "w2_dealt", "w2s_dealt", "x2w"))]
         for t in range(PACK):
-            picked = sbuf.tile([P, J], F32, name="picked%d" % t, tag="picked", bufs=2)
+            picked = sbuf.tile([P, J], F32, name="picked%d" % t, tag="picked", bufs=2, align_bytes=64)
             nc.vector.tensor_copy(picked[:], pa[t][:].indirect(l4[:]))
             nc.vector.memset(pb[t][:], 0.0)
-            diff = sbuf.tile([P, J], F32, name="diff%d" % t, tag="diff")
+            diff = sbuf.tile([P, J], F32, name="diff%d" % t, tag="diff", align_bytes=64)
             nc.vector.tensor_tensor(diff[:], picked[:], b_banks[t // 2][:, t % 2, :], ALU.subtract)
             h1 = sbuf.tile([P, J], F32, name="h1_%d" % t)
             nc.vector.scalar_tensor_tensor(h1[:], diff[:], -1.0, diff[:], ALU.mult, ALU.max)
             put(pb[t], l5[:], h1[:], sb_t[:, t:t + 1])
 
-        hid = [sbuf.tile([P, HALF * PACK], BF16, name="hid%d" % h, align_bytes=64) for h in range(2)]
+        hid_all = sbuf.tile([P, O * PACK], BF16, name="hid_all", tag="diff", align_bytes=64)
+        hid = [hid_all[:, h * HALF * PACK:(h + 1) * HALF * PACK] for h in range(2)]
         for t in range(PACK):
             for h in range(2):
                 nc.scalar.activation(out=hid[h][:, t:HALF * PACK:PACK], in_=pb[t][:].indirect(half(l6, h)), func=COPY)
@@ -177,7 +181,7 @@ def tile_list_relayed_kernel(tc, xt_words, xt_scales, w_words, w_scales, w2_word
         for h in range(2):
             codes = sbuf.tile([P, HALF], U32, name="codes%d" % h, align_bytes=64)
             plane = sbuf.tile([P, HALF], U8, name="plane%d" % h, align_bytes=64)
-            nc.vector.quantize_mx(out=codes[:].bitcast(E4M3), scales=plane[:], in_=hid[h][:])
+            nc.vector.quantize_mx(out=codes[:].bitcast(E4M3), scales=plane[:], in_=hid[h])
             for g in range(2):
                 bank = psum.tile([P, HALF], F32, name="o_bank%d" % g) if h == 0 else psum.tile([P, HALF], F32, name="o_last%d" % g, tag="bank%d" % g)
                 nc.tensor.matmul_mx(out=bank[:], lhsT=wb[:, 2 * P * g:2 * P * (g + 1)].bitcast(E2M1),

@@ -20,6 +20,7 @@ ALU = mybir.AluOpType
 P = 128
 PACK = 4
 HALF = 128
+T_FIRST = 11 * T // 16
 LIST_HALF = HALF // 16
 
 
@@ -39,64 +40,55 @@ def tile_list_relayed_kernel(tc, xt_words, xt_scales, w_words, w_scales, w2_word
         def half(lst, h):
             return lst[:, h * LIST_HALF:(h + 1) * LIST_HALF]
 
-        def zero_plane(width, name, tag, bufs):
-            t = sbuf.tile([P, 2 * width], U8, name=name, tag=tag, bufs=bufs, align_bytes=64)
-            nc.vector.memset(t[0:64, :].bitcast(I32), 0)
-            return t
-
-        def load_plane(plane, scales, width):
-            rows = scales[0].rearrange("(u q r) n -> q r u n", u=2, q=2)
-            for q in range(2):
-                nc.sync.dma_start(plane[32 * q:32 * q + 4, :].bitcast(I32).rearrange("r (u n) -> r u n", u=2),
-                                  rows[q].bitcast(I32))
-
-        def spread_plane(plane, width):
-            nc.vector.tensor_copy(plane[64:128, 0:width].bitcast(I32), plane[0:64, width:2 * width].bitcast(I32))
+        def load_plane(plane, scales):
+            for q in range(4):
+                nc.sync.dma_start(plane[32 * q:32 * q + 4, :].bitcast(I32), scales[0, 4 * q:4 * q + 4, :].bitcast(I32))
 
         xs = sbuf.tile([P, T], U8, name="xs")
         nc.vector.memset(xs[:].bitcast(I32), 0)
-        ws_raw = sbuf.tile([P, R], U8, name="ws_raw")
+        ws_raw = sbuf.tile([P, R], U8, name="ws_raw", align_bytes=64)
         nc.vector.memset(ws_raw[:].bitcast(I32), 0)
 
         l1 = load_list(offs, "l1")
         l3 = load_list(offs3, "l3")
         l4 = load_list(offs4, "l4")
         l5 = load_list(offs5, "l5")
-        w_raw = sbuf.tile([P, 2 * R], U8, name="w_raw")
+        w_raw = sbuf.tile([P, 2 * R], U8, name="w_raw", align_bytes=64)
         nc.scalar.dma_start(w_raw[:].bitcast(I32), w_words[0].bitcast(I32))
         ws_rows = sbuf.tile([4, 4, R // 4], I32, name="ws_rows")
         nc.scalar.dma_start(ws_rows[:], w_scales[0].rearrange("(q r) n -> r q n", q=4).bitcast(I32))
-        xw = sbuf.tile([P, T], U32, name="xw")
-        nc.scalar.dma_start(xw[:].bitcast(I32), xt_words[0].rearrange("p c b -> p (c b)").bitcast(I32))
-        for q in range(4):
-            nc.sync.dma_start(xs[32 * q:32 * q + 4, :].bitcast(I32), xt_scales[0, 4 * q:4 * q + 4, :].bitcast(I32))
-        l2 = load_list(offs2, "l2")
         sa_t = sbuf.tile([P, PACK], F32, name="sa_t")
-        nc.sync.dma_start(sa_t[:], sa.rearrange("(p t) o -> p (t o)", t=PACK))
+        nc.scalar.dma_start(sa_t[:], sa.rearrange("(p t) o -> p (t o)", t=PACK))
+        xw = sbuf.tile([P, T], U32, name="xw")
+        xt_rows = xt_words[0].rearrange("p c b -> p (c b)").bitcast(I32)
+        nc.scalar.dma_start(xw[:, :T_FIRST].bitcast(I32), xt_rows[:, :T_FIRST])
+        l2 = load_list(offs2, "l2")
+        load_plane(xs, xt_scales)
+        l6 = load_list(offs6, "l6")
+        nc.sync.dma_start(xw[:, T_FIRST:].bitcast(I32), xt_rows[:, T_FIRST:])
 
         pa = [sbuf.tile([P, C], F32, name="pa%d" % t) for t in range(PACK)]
         for t in range(PACK):
             nc.vector.memset(pa[t][:], 0.0)
+        pb = [sbuf.tile([P, D], F32, name="pb%d" % t) for t in range(2)]
+        for t in range(2):
+            nc.vector.memset(pb[t][:], 0.0)
 
-        w2s_raw = zero_plane(R, "w2s_raw", "picked", 2)
-        wbs = zero_plane(N, "wbs", "wbs", 1)
-        w2_raw = sbuf.tile([P, R], U32, name="w2_raw", tag="picked", bufs=2, align_bytes=64)
+        w2_raw = sbuf.tile([P, R], U32, name="w2_raw", align_bytes=64)
         nc.sync.dma_start(w2_raw[:].bitcast(I32), w2_words[0].rearrange("p c b -> p (c b)").bitcast(I32))
-        load_plane(w2s_raw, w2_scales, R)
         sb_t = sbuf.tile([P, PACK], F32, name="sb_t")
         nc.sync.dma_start(sb_t[:], sb.rearrange("(p t) o -> p (t o)", t=PACK))
         wb = sbuf.tile([P, 2 * N], U8, name="wb", align_bytes=64)
         nc.sync.dma_start(wb[:].bitcast(I32), wb_words[0].bitcast(I32))
-        load_plane(wbs, wb_scales, N)
-        l6 = load_list(offs6, "l6")
 
         w_dealt = sbuf.tile([P, 2 * R], U8, name="w_dealt", align_bytes=64)
+        nc.scalar.copy(ws_raw[0:4, :].bitcast(U32), ws_rows[:, 0, :].bitcast(U32))
         nc.scalar.copy(w_dealt[:].bitcast(U16).rearrange("p (t m) -> p t m", t=PACK),
                        w_raw[:].bitcast(U16).rearrange("p (m t) -> p t m", t=PACK))
-        for q in range(4):
+        for q in range(1, 4):
             nc.vector.tensor_copy(ws_raw[32 * q:32 * q + 4, :].bitcast(I32), ws_rows[:, q, :])
         ws_dealt = sbuf.tile([P, R], U8, name="ws_dealt", align_bytes=64)
-        nc.vector.tensor_copy(ws_dealt[:].rearrange("p (t m) -> p t m", t=PACK),
+        nc.gpsimd.tensor_copy(ws_dealt[:].rearrange("p (t m) -> p t m", t=PACK),
                               ws_raw[:].rearrange("p (m t) -> p t m", t=PACK))
         x1s = sbuf.tile([P, J], U8, name="x1s", align_bytes=64)
         nc.vector.tensor_copy(x1s[:], xs[:].indirect(l1[:]))
@@ -137,41 +129,43 @@ def tile_list_relayed_kernel(tc, xt_words, xt_scales, w_words, w_scales, w2_word
         for t in range(2):
             put(pa[2 + t], l3[:], a_rest[:, t, :], sa_t[:, 2 + t:3 + t])
 
+        w2s_raw = sbuf.tile([P, R], U8, name="w2s_raw", tag="ws_raw", align_bytes=64)
+        nc.gpsimd.memset(w2s_raw[:].bitcast(I32), 0)
+        load_plane(w2s_raw, w2_scales)
+        wbs = sbuf.tile([P, N], U8, name="wbs", tag="w_raw", align_bytes=64)
+        nc.gpsimd.memset(wbs[:].bitcast(I32), 0)
+        load_plane(wbs, wb_scales)
         x2s = sbuf.tile([P, J], U8, name="x2s", tag="a_first0", align_bytes=64)
         nc.vector.tensor_copy(x2s[:], xs[:].indirect(l2[:]))
         x2w = sbuf.tile([P, J], U32, name="x2w", align_bytes=64)
         nc.vector.tensor_copy(x2w[:], xw[:].indirect(l2[:]))
-        w2_dealt = sbuf.tile([P, R], U32, name="w2_dealt", align_bytes=64)
+        w2_dealt = sbuf.tile([P, R], U32, name="w2_dealt", tag="w_dealt", align_bytes=64)
         nc.vector.tensor_copy(w2_dealt[:].bitcast(I32).rearrange("p (t m) -> p t m", t=PACK),
                               w2_raw[:].bitcast(I32).rearrange("p (m t) -> p t m", t=PACK))
-        spread_plane(w2s_raw, R)
-        w2s_dealt = sbuf.tile([P, R], U8, name="w2s_dealt", align_bytes=64)
-        nc.vector.tensor_copy(w2s_dealt[:].rearrange("p (t m) -> p t m", t=PACK),
-                              w2s_raw[:, 0:R].rearrange("p (m t) -> p t m", t=PACK))
-        spread_plane(wbs, N)
+        w2s_dealt = sbuf.tile([P, R], U8, name="w2s_dealt", tag="ws_dealt", align_bytes=64)
+        nc.gpsimd.tensor_copy(w2s_dealt[:].rearrange("p (t m) -> p t m", t=PACK),
+                              w2s_raw[:].rearrange("p (m t) -> p t m", t=PACK))
         b_banks = []
-        for u in range(2):
-            bank = psum.tile([P, 2, J], F32, name="b_bank%d" % u)
-            for i in range(2):
-                t = 2 * u + i
-                nc.tensor.matmul_mx(out=bank[:, i, :], lhsT=w2_dealt[:, P * t:P * (t + 1)].bitcast(E4M3),
-                                    lhsT_scale=w2s_dealt[:, P * t:P * (t + 1)],
-                                    rhs=x2w[:].bitcast(E5M2), rhs_scale=x2s[:], start=True, stop=True)
+        for t in range(PACK):
+            bank = psum.tile([P, J], F32, name="b_bank%d" % t)
+            nc.tensor.matmul_mx(out=bank[:], lhsT=w2_dealt[:, P * t:P * (t + 1)].bitcast(E4M3),
+                                lhsT_scale=w2s_dealt[:, P * t:P * (t + 1)],
+                                rhs=x2w[:].bitcast(E5M2), rhs_scale=x2s[:], start=True, stop=True)
             b_banks.append(bank)
 
-        pb = [sbuf.tile([P, D], F32, name="pb%d" % t, tag=spent, align_bytes=64)
-              for t, spent in enumerate(("ws_dealt", "w2_dealt", "w2s_dealt", "x2w"))]
         for t in range(PACK):
-            picked = sbuf.tile([P, J], F32, name="picked%d" % t, tag="picked", bufs=2, align_bytes=64)
+            picked = sbuf.tile([P, J], F32, name="picked%d" % t, tag="diff1" if t == 3 else "w2_raw", align_bytes=64)
             nc.vector.tensor_copy(picked[:], pa[t][:].indirect(l4[:]))
-            nc.vector.memset(pb[t][:], 0.0)
-            diff = sbuf.tile([P, J], F32, name="diff%d" % t, tag="diff", align_bytes=64)
-            nc.vector.tensor_tensor(diff[:], picked[:], b_banks[t // 2][:, t % 2, :], ALU.subtract)
+            diff = sbuf.tile([P, J], F32, name="diff%d" % t, align_bytes=64)
+            nc.vector.tensor_tensor(diff[:], picked[:], b_banks[t][:], ALU.subtract)
+            if t >= 2:
+                pb.append(sbuf.tile([P, D], F32, name="pb%d" % t, tag="diff%d" % (2 * t - 4), align_bytes=64))
+                nc.vector.memset(pb[t][:], 0.0)
             h1 = sbuf.tile([P, J], F32, name="h1_%d" % t)
             nc.vector.scalar_tensor_tensor(h1[:], diff[:], -1.0, diff[:], ALU.mult, ALU.max)
             put(pb[t], l5[:], h1[:], sb_t[:, t:t + 1])
 
-        hid_all = sbuf.tile([P, O * PACK], BF16, name="hid_all", tag="diff", align_bytes=64)
+        hid_all = sbuf.tile([P, O * PACK], BF16, name="hid_all", tag="diff3", align_bytes=64)
         hid = [hid_all[:, h * HALF * PACK:(h + 1) * HALF * PACK] for h in range(2)]
         for t in range(PACK):
             for h in range(2):
@@ -183,7 +177,7 @@ def tile_list_relayed_kernel(tc, xt_words, xt_scales, w_words, w_scales, w2_word
             plane = sbuf.tile([P, HALF], U8, name="plane%d" % h, align_bytes=64)
             nc.vector.quantize_mx(out=codes[:].bitcast(E4M3), scales=plane[:], in_=hid[h])
             for g in range(2):
-                bank = psum.tile([P, HALF], F32, name="o_bank%d" % g) if h == 0 else psum.tile([P, HALF], F32, name="o_last%d" % g, tag="bank%d" % g)
+                bank = psum.tile([P, HALF], F32, name="o_bank%d%d" % (h, g), tag="bank%d" % (2 * h + g))
                 nc.tensor.matmul_mx(out=bank[:], lhsT=wb[:, 2 * P * g:2 * P * (g + 1)].bitcast(E2M1),
                                     lhsT_scale=wbs[:, P * g:P * (g + 1)],
                                     rhs=codes[:].bitcast(E4M3), rhs_scale=plane[:], start=True, stop=True)

from contextlib import ExitStack

import concourse.mybir as mybir

K, T, J, R, C, D, O, N = 512, 2048, 256, 512, 512, 512, 256, 256
FLOPS = 2 * (2 * K * R * J + R * N * O)

F32 = mybir.dt.float32
BF16 = mybir.dt.bfloat16
I32 = mybir.dt.int32
U32 = mybir.dt.uint32
U16 = mybir.dt.uint16
U8 = mybir.dt.uint8
E4M3 = mybir.dt.float8_e4m3fn_x4
E5M2 = mybir.dt.float8_e5m2_x4
E2M1 = mybir.dt.float4_e2m1fn_x4
COPY = mybir.ActivationFunctionType.Copy
ALU = mybir.AluOpType

P = 128
PACK = 4
HALF = 128
T_FIRST = 11 * T // 16
LIST_HALF = HALF // 16


def tile_list_relayed_kernel(tc, xt_words, xt_scales, w_words, w_scales, w2_words, w2_scales, sa, sb,
                                 wb_words, wb_scales, offs, offs2, offs3, offs4, offs5, offs6, out):
    nc = tc.nc
    with ExitStack() as ctx:
        lists = ctx.enter_context(tc.tile_pool(name="lists", bufs=1))
        sbuf = ctx.enter_context(tc.tile_pool(name="sbuf", bufs=1))
        psum = ctx.enter_context(tc.psum_pool(name="psum", bufs=1))

        def load_list(src, name):
            t = lists.tile([P, J // 16], U16, name=name)
            nc.sync.dma_start(t[:], src)
            return t

        def half(lst, h):
            return lst[:, h * LIST_HALF:(h + 1) * LIST_HALF]

        def load_plane(plane, scales):
            for q in range(4):
                nc.sync.dma_start(plane[32 * q:32 * q + 4, :].bitcast(I32), scales[0, 4 * q:4 * q + 4, :].bitcast(I32))

        xs = sbuf.tile([P, T], U8, name="xs")
        nc.vector.memset(xs[:].bitcast(I32), 0)
        ws_raw = sbuf.tile([P, R], U8, name="ws_raw", align_bytes=64)
        nc.vector.memset(ws_raw[:].bitcast(I32), 0)

        l1 = load_list(offs, "l1")
        l3 = load_list(offs3, "l3")
        l4 = load_list(offs4, "l4")
        l5 = load_list(offs5, "l5")
        w_raw = sbuf.tile([P, 2 * R], U8, name="w_raw", align_bytes=64)
        nc.scalar.dma_start(w_raw[:].bitcast(I32), w_words[0].bitcast(I32))
        ws_rows = sbuf.tile([4, 4, R // 4], I32, name="ws_rows")
        nc.scalar.dma_start(ws_rows[:], w_scales[0].rearrange("(q r) n -> r q n", q=4).bitcast(I32))
        sa_t = sbuf.tile([P, PACK], F32, name="sa_t")
        nc.scalar.dma_start(sa_t[:], sa.rearrange("(p t) o -> p (t o)", t=PACK))
        xw = sbuf.tile([P, T], U32, name="xw")
        xt_rows = xt_words[0].rearrange("p c b -> p (c b)").bitcast(I32)
        nc.scalar.dma_start(xw[:, :T_FIRST].bitcast(I32), xt_rows[:, :T_FIRST])
        l2 = load_list(offs2, "l2")
        load_plane(xs, xt_scales)
        l6 = load_list(offs6, "l6")
        nc.sync.dma_start(xw[:, T_FIRST:].bitcast(I32), xt_rows[:, T_FIRST:])

        pa = [sbuf.tile([P, C], F32, name="pa%d" % t) for t in range(PACK)]
        for t in range(PACK):
            nc.vector.memset(pa[t][:], 0.0)
        pb = [sbuf.tile([P, D], F32, name="pb%d" % t) for t in range(2)]
        for t in range(2):
            nc.vector.memset(pb[t][:], 0.0)

        w2_raw = sbuf.tile([P, R], U32, name="w2_raw", align_bytes=64)
        nc.sync.dma_start(w2_raw[:].bitcast(I32), w2_words[0].rearrange("p c b -> p (c b)").bitcast(I32))
        sb_t = sbuf.tile([P, PACK], F32, name="sb_t")
        nc.sync.dma_start(sb_t[:], sb.rearrange("(p t) o -> p (t o)", t=PACK))
        wb = sbuf.tile([P, 2 * N], U8, name="wb", align_bytes=64)
        nc.sync.dma_start(wb[:].bitcast(I32), wb_words[0].bitcast(I32))

        w_dealt = sbuf.tile([P, 2 * R], U8, name="w_dealt", align_bytes=64)
        nc.scalar.copy(ws_raw[0:4, :].bitcast(U32), ws_rows[:, 0, :].bitcast(U32))
        nc.scalar.copy(w_dealt[:].bitcast(U16).rearrange("p (t m) -> p t m", t=PACK),
                       w_raw[:].bitcast(U16).rearrange("p (m t) -> p t m", t=PACK))
        for q in range(1, 4):
            nc.vector.tensor_copy(ws_raw[32 * q:32 * q + 4, :].bitcast(I32), ws_rows[:, q, :])
        ws_dealt = sbuf.tile([P, R], U8, name="ws_dealt", align_bytes=64)
        nc.gpsimd.tensor_copy(ws_dealt[:].rearrange("p (t m) -> p t m", t=PACK),
                              ws_raw[:].rearrange("p (m t) -> p t m", t=PACK))
        x1s = sbuf.tile([P, J], U8, name="x1s", align_bytes=64)
        nc.vector.tensor_copy(x1s[:], xs[:].indirect(l1[:]))
        x1w = sbuf.tile([P, J], U32, name="x1w", align_bytes=64)
        for h in range(2):
            nc.vector.tensor_copy(x1w[:, h * HALF:(h + 1) * HALF], xw[:].indirect(half(l1, h)))

        def product_a(dst, t, j0, j1):
            nc.tensor.matmul_mx(out=dst, lhsT=w_dealt[:, 2 * P * t:2 * P * (t + 1)].bitcast(E2M1),
                                lhsT_scale=ws_dealt[:, P * t:P * (t + 1)],
                                rhs=x1w[:, j0:j1].bitcast(E5M2), rhs_scale=x1s[:, j0:j1], start=True, stop=True)

        a_first = []
        for t in range(2):
            bank = psum.tile([P, HALF], F32, name="bank%d" % t)
            product_a(bank[:], t, 0, HALF)
            s = sbuf.tile([P, HALF], F32, name="a_first%d" % t, align_bytes=64)
            nc.scalar.activation(out=s[:], in_=bank[:], func=COPY)
            a_first.append(s)
        bank2 = psum.tile([P, 2, HALF], F32, name="bank2")
        for t in range(2):
            product_a(bank2[:, t, :], t, HALF, J)
        a_second = sbuf.tile([P, 2, HALF], F32, name="a_second")
        nc.vector.tensor_copy(a_second[:], bank2[:])
        bank3 = psum.tile([P, 2, J], F32, name="bank3")
        for t in range(2):
            product_a(bank3[:, t, :], 2 + t, 0, J)
        a_rest = sbuf.tile([P, 2, J], F32, name="a_rest")
        nc.vector.tensor_copy(a_rest[:], bank3[:])

        def put(board, offsets, src, scale):
            nc.scalar.activation(out=board[:].indirect(offsets), in_=src, func=COPY, scale=scale)

        for t in range(2):
            put(pa[t], half(l3, 0), a_first[t][:], sa_t[:, t:t + 1])
        for t in range(2):
            put(pa[t], half(l3, 1), a_second[:, t, :], sa_t[:, t:t + 1])
        for t in range(2):
            put(pa[2 + t], l3[:], a_rest[:, t, :], sa_t[:, 2 + t:3 + t])

        w2s_raw = sbuf.tile([P, R], U8, name="w2s_raw", tag="ws_raw", align_bytes=64)
        nc.gpsimd.memset(w2s_raw[:].bitcast(I32), 0)
        load_plane(w2s_raw, w2_scales)
        wbs = sbuf.tile([P, N], U8, name="wbs", tag="w_raw", align_bytes=64)
        nc.gpsimd.memset(wbs[:].bitcast(I32), 0)
        load_plane(wbs, wb_scales)
        x2s = sbuf.tile([P, J], U8, name="x2s", tag="a_first0", align_bytes=64)
        nc.vector.tensor_copy(x2s[:], xs[:].indirect(l2[:]))
        x2w = sbuf.tile([P, J], U32, name="x2w", align_bytes=64)
        nc.vector.tensor_copy(x2w[:], xw[:].indirect(l2[:]))
        w2_dealt = sbuf.tile([P, R], U32, name="w2_dealt", tag="w_dealt", align_bytes=64)
        nc.vector.tensor_copy(w2_dealt[:].bitcast(I32).rearrange("p (t m) -> p t m", t=PACK),
                              w2_raw[:].bitcast(I32).rearrange("p (m t) -> p t m", t=PACK))
        w2s_dealt = sbuf.tile([P, R], U8, name="w2s_dealt", tag="ws_dealt", align_bytes=64)
        nc.gpsimd.tensor_copy(w2s_dealt[:].rearrange("p (t m) -> p t m", t=PACK),
                              w2s_raw[:].rearrange("p (m t) -> p t m", t=PACK))
        b_banks = []
        for t in range(PACK):
            bank = psum.tile([P, J], F32, name="b_bank%d" % t)
            nc.tensor.matmul_mx(out=bank[:], lhsT=w2_dealt[:, P * t:P * (t + 1)].bitcast(E4M3),
                                lhsT_scale=w2s_dealt[:, P * t:P * (t + 1)],
                                rhs=x2w[:].bitcast(E5M2), rhs_scale=x2s[:], start=True, stop=True)
            b_banks.append(bank)

        for t in range(PACK):
            picked = sbuf.tile([P, J], F32, name="picked%d" % t, tag="diff1" if t == 3 else "w2_raw", align_bytes=64)
            nc.vector.tensor_copy(picked[:], pa[t][:].indirect(l4[:]))
            diff = sbuf.tile([P, J], F32, name="diff%d" % t, align_bytes=64)
            nc.vector.tensor_tensor(diff[:], picked[:], b_banks[t][:], ALU.subtract)
            if t >= 2:
                pb.append(sbuf.tile([P, D], F32, name="pb%d" % t, tag="diff%d" % (2 * t - 4), align_bytes=64))
                nc.vector.memset(pb[t][:], 0.0)
            h1 = sbuf.tile([P, J], F32, name="h1_%d" % t)
            nc.vector.scalar_tensor_tensor(h1[:], diff[:], -1.0, diff[:], ALU.mult, ALU.max)
            put(pb[t], l5[:], h1[:], sb_t[:, t:t + 1])

        hid_all = sbuf.tile([P, O * PACK], BF16, name="hid_all", tag="diff3", align_bytes=64)
        hid = [hid_all[:, h * HALF * PACK:(h + 1) * HALF * PACK] for h in range(2)]
        for t in range(PACK):
            for h in range(2):
                nc.scalar.activation(out=hid[h][:, t:HALF * PACK:PACK], in_=pb[t][:].indirect(half(l6, h)), func=COPY)

        out_rows = out.rearrange("(g p) o -> p g o", p=P)
        for h in range(2):
            codes = sbuf.tile([P, HALF], U32, name="codes%d" % h, align_bytes=64)
            plane = sbuf.tile([P, HALF], U8, name="plane%d" % h, align_bytes=64)
            nc.vector.quantize_mx(out=codes[:].bitcast(E4M3), scales=plane[:], in_=hid[h])
            for g in range(2):
                bank = psum.tile([P, HALF], F32, name="o_bank%d%d" % (h, g), tag="bank%d" % (2 * h + g))
                nc.tensor.matmul_mx(out=bank[:], lhsT=wb[:, 2 * P * g:2 * P * (g + 1)].bitcast(E2M1),
                                    lhsT_scale=wbs[:, P * g:P * (g + 1)],
                                    rhs=codes[:].bitcast(E4M3), rhs_scale=plane[:], start=True, stop=True)
                res = sbuf.tile([P, HALF], F32, name="res%d%d" % (h, g))
                if g == 1:
                    nc.scalar.copy(res[:], bank[:])
                    nc.scalar.dma_start(out_rows[:, g, h * HALF:(h + 1) * HALF], res[:])
                else:
                    nc.vector.tensor_copy(res[:], bank[:])
                    nc.sync.dma_start(out_rows[:, g, h * HALF:(h + 1) * HALF], res[:])
